import numpy as np
import ml_dtypes


def mxq(x, axis, fmt="e4m3"):
    dtype, down = {"e4m3": (ml_dtypes.float8_e4m3fn, 7), "e5m2": (ml_dtypes.float8_e5m2, 14)}[fmt]
    v = np.moveaxis(np.asarray(x, np.float32).astype(ml_dtypes.bfloat16).astype(np.float64), axis, -1)
    blocks = v.reshape(v.shape[:-1] + (-1, 32))
    amax = np.abs(blocks).max(-1, keepdims=True)
    byte = np.maximum(np.where(amax > 0, np.frexp(amax)[1] - 1 + 127, 0) - down, 1)
    scale = np.exp2(byte - 127.0)
    codes = (blocks / scale).astype(np.float32).astype(dtype).astype(np.float64)
    return np.moveaxis((codes * scale).reshape(v.shape), -1, axis)


WIDE = False


def mx_kscale(k, group=512):
    if not WIDE:
        return np.ones(k)
    levels = np.array([10, -10, 5, -5, 0])
    if group != 512:
        return np.exp2(np.random.permutation(np.resize(levels, k // group))).repeat(group)
    if k % 512:
        return np.exp2(np.random.permutation(np.resize(levels, k // 32))).repeat(32)
    a = np.empty((k // 512, 16))
    for p in range(k // 512):
        a[p, :8] = np.random.permutation(np.resize(levels, 8))
        for g in range(8):
            far = levels[np.abs(levels - a[p, g]) >= 10]
            a[p, g + 8] = far[np.random.randint(len(far))]
    return np.exp2(a.ravel()).repeat(32)


def f64(x):
    return np.asarray(x).astype(np.float64)


E2M1 = np.array([0.0, 0.5, 1.0, 1.5, 2.0, 3.0, 4.0, 6.0, -0.0, -0.5, -1.0, -1.5, -2.0, -3.0, -4.0, -6.0])


def pack_group(w):
    k, n = w.shape
    w = f64(np.asarray(w, np.float32).astype(ml_dtypes.bfloat16)).reshape(k // 32, 32, n)
    amax = np.abs(w).max(1)
    mant, ex = np.frexp(amax / 6.0)
    byte = np.clip(np.where(amax > 0, np.where(mant > 0.5, ex, ex - 1) + 127, 1), 1, 254)
    scaled = (w * np.exp2(127.0 - byte)[:, None, :]).reshape(k, n).astype(np.float32)
    c = np.ascontiguousarray(scaled.reshape(k // 4, 4, n).transpose(0, 2, 1)).astype(ml_dtypes.float4_e2m1fn).view(np.uint8) & 0xF
    return np.ascontiguousarray((c[..., 0::2] | (c[..., 1::2] << 4)).reshape(k // 4, 2 * n)), byte.astype(np.uint8)


def unpack_group(words, scales):
    p, n = words.shape[0], scales.shape[1]
    words = np.ascontiguousarray(words).reshape(p, n, 2)
    nib = np.empty((p, n, 4), np.uint8)
    nib[..., 0::2] = words & 0xF
    nib[..., 1::2] = words >> 4
    return E2M1[nib].transpose(0, 2, 1).reshape(4 * p, n) * np.repeat(np.exp2(scales.astype(np.float64) - 127.0), 32, axis=0)


G, D, M, O, N = 2, 256, 256, 256, 512


def setup_inputs():
    n = np.random.standard_normal
    s_d = mx_kscale(D, 0)
    s_o = mx_kscale(O, 0)
    w1_ = [pack_group(w) for w in n((G, D, M)) / np.sqrt(D) / s_d[:, None]]
    w2_ = [pack_group(w) for w in n((G, D, M)) / np.sqrt(D) / s_d[:, None]]
    wo_ = [pack_group(w) for w in n((G, O, M)) / np.sqrt(O) / s_o[:, None]]
    return {
        "x": (n((G, D, N)) * s_d[:, None]).astype(np.float32),
        "w1_words": np.stack([w[0] for w in w1_]),
        "w1_scales": np.stack([w[1] for w in w1_]),
        "w2_words": np.stack([w[0] for w in w2_]),
        "w2_scales": np.stack([w[1] for w in w2_]),
        "ra": (np.random.uniform(0.3, 1.5, (G, M, 1))).astype(np.float32),
        "wo_words": np.stack([w[0] for w in wo_]),
        "wo_scales": np.stack([w[1] for w in wo_]),
        "dy": (n((G, O, N)) * s_o[:, None]).astype(np.float32),
        "old": (0.3 * n((G, M, N))).astype(np.float32),
    }


def reference(x, w1_words, w1_scales, w2_words, w2_scales, ra, wo_words, wo_scales, dy, old):
    w1 = np.stack([unpack_group(w1_words[g], w1_scales[g]) for g in range(G)])
    xq = mxq(f64(x), 1, "e4m3")
    z1 = w1.transpose(0, 2, 1) @ xq
    w2 = np.stack([unpack_group(w2_words[g], w2_scales[g]) for g in range(G)])
    z2 = w2.transpose(0, 2, 1) @ xq
    nn = np.sqrt(np.square(z1) + np.square(z2) + f64(ra))
    wo = np.stack([unpack_group(wo_words[g], wo_scales[g]) for g in range(G)])
    dyq = mxq(f64(dy), 1, "e4m3")
    c0 = wo.transpose(0, 2, 1) @ dyq
    dnn = c0 * z1 / np.square(nn) * (-1.0)
    dz1 = c0 / nn + dnn * 0.5 / np.sqrt(np.square(z1) + np.square(z2) + f64(ra)) * z1 * 2.0
    y = dz1 + f64(old)
    return y

@@ -1,0 +1,158 @@
+from contextlib import ExitStack
+
+import concourse.mybir as mybir
+
+G, D, M, N = 2, 256, 256, 512
+FLOPS = 3 * 2 * G * D * M * N
+
+F32 = mybir.dt.float32
+BF16 = mybir.dt.bfloat16
+I32 = mybir.dt.int32
+U32 = mybir.dt.uint32
+U8 = mybir.dt.uint8
+FP8X4 = mybir.dt.float8_e4m3fn_x4
+FP4X4 = mybir.dt.float4_e2m1fn_x4
+ACT = mybir.ActivationFunctionType
+ALU = mybir.AluOpType
+
+P = 128
+PACK = 4
+ROWS = D // PACK
+HALVES = M // P
+TILES = G * HALVES
+X_VECTOR_COLUMNS = 344
+
+
+def tile_rows_bsphere_kernel(tc, x, w1_words, w1_scales, w2_words, w2_scales, ra, wo_words, wo_scales, dy, old, out):
+    nc = tc.nc
+    with ExitStack() as ctx:
+        sb = ctx.enter_context(tc.tile_pool(name="sb", bufs=1))
+        ps = ctx.enter_context(tc.psum_pool(name="ps", bufs=1))
+        ctx.enter_context(tc.manual_schedule())
+
+        x_raw = sb.tile([P, PACK, N], F32, name="x_raw")
+        dy_raw = sb.tile([P, PACK, N], F32, name="dy_raw")
+        old_sb = sb.tile([P, TILES, N], F32, name="old_sb")
+        ra_sb = sb.tile([P, TILES, 8], F32, name="ra_sb")
+        rho = sb.tile([P, TILES], F32, name="rho")
+        w_scales = sb.tile([P, 3 * M], U8, name="w_scales", align_bytes=64)
+        w1_sb = sb.tile([P, 2 * M], U8, name="w1_sb", align_bytes=64)
+        w2_sb = sb.tile([P, 2 * M], U8, name="w2_sb", align_bytes=64)
+        wo_sb = sb.tile([P, 2 * M], U8, name="wo_sb", align_bytes=64)
+        w1_plane, w2_plane, wo_plane = (w_scales[:, k * M : (k + 1) * M] for k in range(3))
+
+        def load_rows(raw, src):
+            nc.sync.dma_start(out=raw[:], in_=src.rearrange("g (p j) n -> (g p) j n", j=PACK))
+
+        def load_words(queue, tile, words):
+            queue.dma_start(out=tile[:].bitcast(I32), in_=words.rearrange("g p b -> (g p) b").bitcast(I32))
+
+        def load_plane(queue, plane, scales):
+            rows = scales.rearrange("g t m -> (g t) m").bitcast(I32)
+            for q in range(4):
+                queue.dma_start(out=plane[32 * q : 32 * q + 4, :].bitcast(I32), in_=rows[4 * q : 4 * q + 4, :])
+
+        nc.vector.memset(w_scales[:].bitcast(I32), 0)
+        load_rows(x_raw, x)
+        with nc.allow_non_contiguous_dma(reason="one offset a partition"):
+            nc.scalar.dma_start(out=ra_sb[:, :, 0:1], in_=ra.rearrange("g (h p) o -> p (g h) o", p=P))
+        load_words(nc.gpsimd, w2_sb, w2_words)
+        load_plane(nc.gpsimd, w2_plane, w2_scales)
+        load_plane(nc.sync, w1_plane, w1_scales)
+        load_words(nc.sync, w1_sb, w1_words)
+        load_rows(dy_raw, dy)
+        load_plane(nc.sync, wo_plane, wo_scales)
+        load_words(nc.sync, wo_sb, wo_words)
+        nc.sync.dma_start(out=old_sb[:], in_=old.rearrange("g (h p) n -> p (g h) n", p=P))
+
+        nc.scalar.activation(out=rho[:], in_=ra_sb[:, :, 0], func=ACT.Abs_reciprocal_sqrt)
+
+        def interleave(copy, grouped, raw, c0, c1):
+            copy(
+                out=grouped[:, c0:c1, :].rearrange("p (c i) j -> p c j i", i=4),
+                in_=raw[:, :, c0:c1].rearrange("p j (c i) -> p c j i", i=4),
+            )
+
+        def quantise(grouped, name):
+            codes = sb.tile([P, N], U32, name=name + "_codes", align_bytes=64)
+            scales = sb.tile([P, N], U8, name=name + "_scales", align_bytes=64)
+            nc.vector.quantize_mx(out=codes[:].bitcast(FP8X4), scales=scales[:], in_=grouped[:].rearrange("p n j -> p (n j)"))
+            return codes, scales
+
+        x_grouped = sb.tile([P, N, PACK], BF16, name="x_grouped", align_bytes=64)
+        interleave(nc.vector.tensor_copy, x_grouped, x_raw, 0, X_VECTOR_COLUMNS)
+        interleave(nc.scalar.copy, x_grouped, x_raw, X_VECTOR_COLUMNS, N)
+        x_mx = quantise(x_grouped, "x")
+        dy_grouped = sb.tile([P, N, PACK], BF16, name="dy_grouped", align_bytes=64)
+        interleave(nc.vector.tensor_copy, dy_grouped, dy_raw, 0, N)
+        dy_mx = quantise(dy_grouped, "dy")
+
+        def place(i):
+            return i % G, i // G
+
+        def product(bank, i, words, plane, moving):
+            g, h = place(i)
+            rows = slice(ROWS * g, ROWS * (g + 1))
+            codes, scales = moving
+            nc.tensor.matmul_mx(
+                out=bank[:],
+                lhsT=words[rows, 2 * P * h : 2 * P * (h + 1)].bitcast(FP4X4),
+                lhsT_scale=plane[rows, P * h : P * (h + 1)],
+                rhs=codes[rows, :].bitcast(FP8X4),
+                rhs_scale=scales[rows, :],
+                start=True,
+                stop=True,
+            )
+
+        z1_bank = [ps.tile([P, N], F32, name="z1_bank%d" % i) for i in range(TILES)]
+        z2_bank = [ps.tile([P, N], F32, name="z2_bank%d" % i) for i in range(TILES)]
+
+        def work(name):
+            return [sb.tile([P, N], F32, name="%s%d" % (name, i)) for i in range(TILES)]
+
+        sq1, sq2, radius2, root, unit, grad, unit2, minus, result = (
+            work(name) for name in ("sq1", "sq2", "radius2", "root", "unit", "grad", "unit2", "minus", "result")
+        )
+
+        def rho_of(i):
+            g, h = place(i)
+            return rho[:, HALVES * g + h : HALVES * g + h + 1]
+
+        def forward(i):
+            product(z1_bank[i], i, w1_sb, w1_plane, x_mx)
+            product(z2_bank[i], i, w2_sb, w2_plane, x_mx)
+
+        def squares(i):
+            nc.scalar.activation(out=sq1[i][:], in_=z1_bank[i][:], func=ACT.Square, scale=rho_of(i))
+            nc.scalar.activation(out=sq2[i][:], in_=z2_bank[i][:], func=ACT.Square, scale=rho_of(i))
+            nc.vector.tensor_tensor(out=radius2[i][:], in0=sq1[i][:], in1=sq2[i][:], op=ALU.add)
+
+        def roots(i):
+            nc.scalar.activation(out=root[i][:], in_=radius2[i][:], func=ACT.Abs_reciprocal_sqrt, bias=1.0)
+            for dst, bank in ((unit, z1_bank), (grad, z2_bank)):
+                nc.vector.scalar_tensor_tensor(
+                    out=dst[i][:], in0=bank[i][:], scalar=rho_of(i), in1=root[i][:], op0=ALU.mult, op1=ALU.mult
+                )
+
+        def finish(i):
+            g, h = place(i)
+            nc.scalar.activation(out=unit2[i][:], in_=unit[i][:], func=ACT.Square)
+            nc.vector.scalar_tensor_tensor(
+                out=minus[i][:], in0=unit2[i][:], scalar=1.0, in1=grad[i][:], op0=ALU.subtract, op1=ALU.mult
+            )
+            engine = nc.gpsimd if i < TILES - 1 else nc.vector
+            engine.tensor_tensor(out=result[i][:], in0=old_sb[:, HALVES * g + h, :], in1=minus[i][:], op=ALU.subtract)
+            nc.sync.dma_start(out=out[g, P * h : P * (h + 1), :], in_=result[i][:])
+
+        forward(0)
+        forward(1)
+        for step in range(TILES + 2):
+            if step < TILES:
+                squares(step)
+            if 1 <= step < TILES - 1:
+                forward(step + 1)
+            if step >= 2:
+                finish(step - 2)
+            if 1 <= step <= TILES:
+                product(z2_bank[step - 1], step - 1, wo_sb, wo_plane, dy_mx)
+                roots(step - 1)

@@ -20,7 +20,8 @@ PACK = 4
 ROWS = D // PACK
 HALVES = M // P
 TILES = G * HALVES
-X_VECTOR_COLUMNS = 344
+PART = N // 2
+VECTOR_COLUMNS = 168
 
 
 def tile_rows_bsphere_kernel(tc, x, w1_words, w1_scales, w2_words, w2_scales, ra, wo_words, wo_scales, dy, old, out):
@@ -30,10 +31,11 @@ def tile_rows_bsphere_kernel(tc, x, w1_words, w1_scales, w2_words, w2_scales, ra
         ps = ctx.enter_context(tc.psum_pool(name="ps", bufs=1))
         ctx.enter_context(tc.manual_schedule())
 
-        x_raw = sb.tile([P, PACK, N], F32, name="x_raw")
-        dy_raw = sb.tile([P, PACK, N], F32, name="dy_raw")
+        x_raw = [sb.tile([P, PACK, PART], F32, name="x_raw%d" % k) for k in range(2)]
+        dy_raw = [sb.tile([P, PACK, PART], F32, name="dy_raw%d" % k) for k in range(2)]
         old_sb = sb.tile([P, TILES, N], F32, name="old_sb")
-        ra_sb = sb.tile([P, TILES, 8], F32, name="ra_sb")
+        ra_rows = sb.tile([P, P], F32, name="ra_rows", align_bytes=64)
+        ra_cols = sb.tile([P, P], F32, name="ra_cols", align_bytes=64)
         rho = sb.tile([P, TILES], F32, name="rho")
         w_scales = sb.tile([P, 3 * M], U8, name="w_scales", align_bytes=64)
         w1_sb = sb.tile([P, 2 * M], U8, name="w1_sb", align_bytes=64)
@@ -42,30 +44,38 @@ def tile_rows_bsphere_kernel(tc, x, w1_words, w1_scales, w2_words, w2_scales, ra
         w1_plane, w2_plane, wo_plane = (w_scales[:, k * M : (k + 1) * M] for k in range(3))
 
         def load_rows(raw, src):
-            nc.sync.dma_start(out=raw[:], in_=src.rearrange("g (p j) n -> (g p) j n", j=PACK))
+            rows = src.rearrange("g (p j) n -> (g p) j n", j=PACK)
+            for part in range(2):
+                nc.sync.dma_start(out=raw[part][:], in_=rows[:, :, part * PART : (part + 1) * PART])
 
         def load_words(queue, tile, words):
             queue.dma_start(out=tile[:].bitcast(I32), in_=words.rearrange("g p b -> (g p) b").bitcast(I32))
 
-        def load_plane(queue, plane, scales):
+        def load_plane(queue, plane, scales, quadrants):
             rows = scales.rearrange("g t m -> (g t) m").bitcast(I32)
-            for q in range(4):
+            for q in quadrants:
                 queue.dma_start(out=plane[32 * q : 32 * q + 4, :].bitcast(I32), in_=rows[4 * q : 4 * q + 4, :])
 
+        nc.vector.memset(ra_rows[:], 0.0)
         nc.vector.memset(w_scales[:].bitcast(I32), 0)
-        load_rows(x_raw, x)
-        with nc.allow_non_contiguous_dma(reason="one offset a partition"):
-            nc.scalar.dma_start(out=ra_sb[:, :, 0:1], in_=ra.rearrange("g (h p) o -> p (g h) o", p=P))
-        load_words(nc.gpsimd, w2_sb, w2_words)
-        load_plane(nc.gpsimd, w2_plane, w2_scales)
-        load_plane(nc.sync, w1_plane, w1_scales)
         load_words(nc.sync, w1_sb, w1_words)
+        nc.sync.dma_start(
+            out=ra_rows[0:P:32, :].rearrange("q (c i) -> q c i", i=32),
+            in_=ra.rearrange("g (h q i) o -> q (g h) (i o)", q=4, i=32),
+        )
+        load_rows(x_raw, x)
+        load_words(nc.sync, w2_sb, w2_words)
+        load_plane(nc.sync, w1_plane, w1_scales, range(0, 2))
+        load_plane(nc.sync, w2_plane, w2_scales, range(0, 2))
         load_rows(dy_raw, dy)
-        load_plane(nc.sync, wo_plane, wo_scales)
+        load_plane(nc.sync, w1_plane, w1_scales, range(2, 4))
+        load_plane(nc.sync, w2_plane, w2_scales, range(2, 4))
         load_words(nc.sync, wo_sb, wo_words)
+        load_plane(nc.sync, wo_plane, wo_scales, range(4))
         nc.sync.dma_start(out=old_sb[:], in_=old.rearrange("g (h p) n -> p (g h) n", p=P))
 
-        nc.scalar.activation(out=rho[:], in_=ra_sb[:, :, 0], func=ACT.Abs_reciprocal_sqrt)
+        nc.vector.transpose(out=ra_cols[:], in_=ra_rows[:])
+        nc.scalar.activation(out=rho[:], in_=ra_cols[:, 0:P:32], func=ACT.Abs_reciprocal_sqrt)
 
         def interleave(copy, grouped, raw, c0, c1):
             copy(
@@ -73,19 +83,27 @@ def tile_rows_bsphere_kernel(tc, x, w1_words, w1_scales, w2_words, w2_scales, ra
                 in_=raw[:, :, c0:c1].rearrange("p j (c i) -> p c j i", i=4),
             )
 
-        def quantise(grouped, name):
+        def mx_operand(name):
             codes = sb.tile([P, N], U32, name=name + "_codes", align_bytes=64)
             scales = sb.tile([P, N], U8, name=name + "_scales", align_bytes=64)
-            nc.vector.quantize_mx(out=codes[:].bitcast(FP8X4), scales=scales[:], in_=grouped[:].rearrange("p n j -> p (n j)"))
             return codes, scales
 
-        x_grouped = sb.tile([P, N, PACK], BF16, name="x_grouped", align_bytes=64)
-        interleave(nc.vector.tensor_copy, x_grouped, x_raw, 0, X_VECTOR_COLUMNS)
-        interleave(nc.scalar.copy, x_grouped, x_raw, X_VECTOR_COLUMNS, N)
-        x_mx = quantise(x_grouped, "x")
-        dy_grouped = sb.tile([P, N, PACK], BF16, name="dy_grouped", align_bytes=64)
-        interleave(nc.vector.tensor_copy, dy_grouped, dy_raw, 0, N)
-        dy_mx = quantise(dy_grouped, "dy")
+        def quantise(operand, raw, name, part, vector_columns):
+            codes, scales = operand
+            cols = slice(part * PART, (part + 1) * PART)
+            grouped = sb.tile([P, PART, PACK], BF16, name="%s_grouped%d" % (name, part), align_bytes=64)
+            interleave(nc.vector.tensor_copy, grouped, raw[part], 0, vector_columns)
+            if vector_columns < PART:
+                interleave(nc.scalar.copy, grouped, raw[part], vector_columns, PART)
+            nc.vector.quantize_mx(
+                out=codes[:, cols].bitcast(FP8X4), scales=scales[:, cols], in_=grouped[:].rearrange("p n j -> p (n j)")
+            )
+
+        x_mx, dy_mx = mx_operand("x"), mx_operand("dy")
+        quantise(x_mx, x_raw, "x", 0, VECTOR_COLUMNS)
+        quantise(x_mx, x_raw, "x", 1, VECTOR_COLUMNS)
+        quantise(dy_mx, dy_raw, "dy", 0, VECTOR_COLUMNS)
+        quantise(dy_mx, dy_raw, "dy", 1, PART)
 
         def place(i):
             return i % G, i // G
@@ -137,12 +155,19 @@ def tile_rows_bsphere_kernel(tc, x, w1_words, w1_scales, w2_words, w2_scales, ra
         def finish(i):
             g, h = place(i)
             nc.scalar.activation(out=unit2[i][:], in_=unit[i][:], func=ACT.Square)
-            nc.vector.scalar_tensor_tensor(
-                out=minus[i][:], in0=unit2[i][:], scalar=1.0, in1=grad[i][:], op0=ALU.subtract, op1=ALU.mult
-            )
-            engine = nc.gpsimd if i < TILES - 1 else nc.vector
-            engine.tensor_tensor(out=result[i][:], in0=old_sb[:, HALVES * g + h, :], in1=minus[i][:], op=ALU.subtract)
-            nc.sync.dma_start(out=out[g, P * h : P * (h + 1), :], in_=result[i][:])
+            last = i == TILES - 1
+            pieces = [slice(0, PART), slice(PART, N)] if last else [slice(0, N)]
+            for cols in pieces:
+                nc.vector.scalar_tensor_tensor(
+                    out=minus[i][:, cols], in0=unit2[i][:, cols], scalar=1.0, in1=grad[i][:, cols],
+                    op0=ALU.subtract, op1=ALU.mult,
+                )
+            engine = nc.vector if last else nc.gpsimd
+            for cols in pieces:
+                engine.tensor_tensor(
+                    out=result[i][:, cols], in0=old_sb[:, HALVES * g + h, cols], in1=minus[i][:, cols], op=ALU.subtract
+                )
+                nc.sync.dma_start(out=out[g, P * h : P * (h + 1), cols], in_=result[i][:, cols])
 
         forward(0)
         forward(1)

@@ -147,24 +147,27 @@ def tile_rows_bsphere_kernel(tc, x, w1_words, w1_scales, w2_words, w2_scales, ra
 
         def roots(i):
             nc.scalar.activation(out=root[i][:], in_=radius2[i][:], func=ACT.Abs_reciprocal_sqrt, bias=1.0)
-            for dst, bank in ((unit, z1_bank), (grad, z2_bank)):
-                nc.vector.scalar_tensor_tensor(
-                    out=dst[i][:], in0=bank[i][:], scalar=rho_of(i), in1=root[i][:], op0=ALU.mult, op1=ALU.mult
-                )
 
-        def finish(i):
-            g, h = place(i)
+        def times_root(dst, bank, i):
+            nc.vector.scalar_tensor_tensor(
+                out=dst[i][:], in0=bank[i][:], scalar=rho_of(i), in1=root[i][:], op0=ALU.mult, op1=ALU.mult
+            )
+
+        def pieces(i):
+            return [slice(0, PART), slice(PART, N)] if i == TILES - 1 else [slice(0, N)]
+
+        def correction(i):
             nc.scalar.activation(out=unit2[i][:], in_=unit[i][:], func=ACT.Square)
-            last = i == TILES - 1
-            pieces = [slice(0, PART), slice(PART, N)] if last else [slice(0, N)]
-            for cols in pieces:
+            for cols in pieces(i):
                 nc.vector.scalar_tensor_tensor(
                     out=minus[i][:, cols], in0=unit2[i][:, cols], scalar=1.0, in1=grad[i][:, cols],
                     op0=ALU.subtract, op1=ALU.mult,
                 )
-            engine = nc.vector if last else nc.gpsimd
-            for cols in pieces:
-                engine.tensor_tensor(
+
+        def finish(i):
+            g, h = place(i)
+            for cols in pieces(i):
+                nc.vector.tensor_tensor(
                     out=result[i][:, cols], in0=old_sb[:, HALVES * g + h, cols], in1=minus[i][:, cols], op=ALU.subtract
                 )
                 nc.sync.dma_start(out=out[g, P * h : P * (h + 1), cols], in_=result[i][:, cols])
@@ -177,7 +180,12 @@ def tile_rows_bsphere_kernel(tc, x, w1_words, w1_scales, w2_words, w2_scales, ra
             if 1 <= step < TILES - 1:
                 forward(step + 1)
             if step >= 2:
-                finish(step - 2)
+                correction(step - 2)
             if 1 <= step <= TILES:
                 product(z2_bank[step - 1], step - 1, wo_sb, wo_plane, dy_mx)
                 roots(step - 1)
+                times_root(unit, z1_bank, step - 1)
+            if step >= 2:
+                finish(step - 2)
+            if 1 <= step <= TILES:
+                times_root(grad, z2_bank, step - 1)

@@ -21,7 +21,7 @@ ROWS = D // PACK
 HALVES = M // P
 TILES = G * HALVES
 PART = N // 2
-VECTOR_COLUMNS = 168
+VECTOR_COLUMNS = 144
 
 
 def tile_rows_bsphere_kernel(tc, x, w1_words, w1_scales, w2_words, w2_scales, ra, wo_words, wo_scales, dy, old, out):
@@ -33,7 +33,7 @@ def tile_rows_bsphere_kernel(tc, x, w1_words, w1_scales, w2_words, w2_scales, ra
 
         x_raw = [sb.tile([P, PACK, PART], F32, name="x_raw%d" % k) for k in range(2)]
         dy_raw = [sb.tile([P, PACK, PART], F32, name="dy_raw%d" % k) for k in range(2)]
-        old_sb = sb.tile([P, TILES, N], F32, name="old_sb")
+        old_sb = [sb.tile([P, HALVES, N], F32, name="old_sb%d" % g) for g in range(G)]
         ra_rows = sb.tile([P, P], F32, name="ra_rows", align_bytes=64)
         ra_cols = sb.tile([P, P], F32, name="ra_cols", align_bytes=64)
         rho = sb.tile([P, TILES], F32, name="rho")
@@ -43,39 +43,42 @@ def tile_rows_bsphere_kernel(tc, x, w1_words, w1_scales, w2_words, w2_scales, ra
         wo_sb = sb.tile([P, 2 * M], U8, name="wo_sb", align_bytes=64)
         w1_plane, w2_plane, wo_plane = (w_scales[:, k * M : (k + 1) * M] for k in range(3))
 
-        def load_rows(raw, src):
+        def load_rows(raw, src, part):
             rows = src.rearrange("g (p j) n -> (g p) j n", j=PACK)
-            for part in range(2):
-                nc.sync.dma_start(out=raw[part][:], in_=rows[:, :, part * PART : (part + 1) * PART])
+            nc.sync.dma_start(out=raw[part][:], in_=rows[:, :, part * PART : (part + 1) * PART])
 
-        def load_words(queue, tile, words):
-            queue.dma_start(out=tile[:].bitcast(I32), in_=words.rearrange("g p b -> (g p) b").bitcast(I32))
+        def load_words(tile, words):
+            nc.sync.dma_start(out=tile[:].bitcast(I32), in_=words.rearrange("g p b -> (g p) b").bitcast(I32))
 
-        def load_plane(queue, plane, scales, quadrants):
+        def load_plane(plane, scales, g):
             rows = scales.rearrange("g t m -> (g t) m").bitcast(I32)
-            for q in quadrants:
-                queue.dma_start(out=plane[32 * q : 32 * q + 4, :].bitcast(I32), in_=rows[4 * q : 4 * q + 4, :])
+            for q in (2 * g, 2 * g + 1):
+                nc.sync.dma_start(out=plane[32 * q : 32 * q + 4, :].bitcast(I32), in_=rows[4 * q : 4 * q + 4, :])
+
+        def load_old(g):
+            nc.sync.dma_start(out=old_sb[g][:], in_=old[g].rearrange("(h p) n -> p h n", p=P))
 
         nc.vector.memset(ra_rows[:], 0.0)
         nc.vector.memset(w_scales[:].bitcast(I32), 0)
-        load_words(nc.sync, w1_sb, w1_words)
+        load_rows(x_raw, x, 0)
         nc.sync.dma_start(
             out=ra_rows[0:P:32, :].rearrange("q (c i) -> q c i", i=32),
             in_=ra.rearrange("g (h q i) o -> q (g h) (i o)", q=4, i=32),
         )
-        load_rows(x_raw, x)
-        load_words(nc.sync, w2_sb, w2_words)
-        load_plane(nc.sync, w1_plane, w1_scales, range(0, 2))
-        load_plane(nc.sync, w2_plane, w2_scales, range(0, 2))
-        load_rows(dy_raw, dy)
-        load_plane(nc.sync, w1_plane, w1_scales, range(2, 4))
-        load_plane(nc.sync, w2_plane, w2_scales, range(2, 4))
-        load_words(nc.sync, wo_sb, wo_words)
-        load_plane(nc.sync, wo_plane, wo_scales, range(4))
-        nc.sync.dma_start(out=old_sb[:], in_=old.rearrange("g (h p) n -> p (g h) n", p=P))
-
-        nc.vector.transpose(out=ra_cols[:], in_=ra_rows[:])
-        nc.scalar.activation(out=rho[:], in_=ra_cols[:, 0:P:32], func=ACT.Abs_reciprocal_sqrt)
+        load_rows(x_raw, x, 1)
+        load_words(w1_sb, w1_words)
+        load_plane(w1_plane, w1_scales, 0)
+        load_words(w2_sb, w2_words)
+        load_plane(w2_plane, w2_scales, 0)
+        load_rows(dy_raw, dy, 0)
+        load_rows(dy_raw, dy, 1)
+        load_words(wo_sb, wo_words)
+        load_plane(wo_plane, wo_scales, 0)
+        load_plane(w1_plane, w1_scales, 1)
+        load_plane(w2_plane, w2_scales, 1)
+        load_old(0)
+        load_plane(wo_plane, wo_scales, 1)
+        load_old(1)
 
         def interleave(copy, grouped, raw, c0, c1):
             copy(
@@ -88,25 +91,31 @@ def tile_rows_bsphere_kernel(tc, x, w1_words, w1_scales, w2_words, w2_scales, ra
             scales = sb.tile([P, N], U8, name=name + "_scales", align_bytes=64)
             return codes, scales
 
-        def quantise(operand, raw, name, part, vector_columns):
-            codes, scales = operand
-            cols = slice(part * PART, (part + 1) * PART)
+        def round_part(raw, name, part, vector_columns):
             grouped = sb.tile([P, PART, PACK], BF16, name="%s_grouped%d" % (name, part), align_bytes=64)
             interleave(nc.vector.tensor_copy, grouped, raw[part], 0, vector_columns)
             if vector_columns < PART:
                 interleave(nc.scalar.copy, grouped, raw[part], vector_columns, PART)
+            return grouped
+
+        def quantise(operand, grouped, part):
+            codes, scales = operand
+            cols = slice(part * PART, (part + 1) * PART)
             nc.vector.quantize_mx(
                 out=codes[:, cols].bitcast(FP8X4), scales=scales[:, cols], in_=grouped[:].rearrange("p n j -> p (n j)")
             )
 
         x_mx, dy_mx = mx_operand("x"), mx_operand("dy")
-        quantise(x_mx, x_raw, "x", 0, VECTOR_COLUMNS)
-        quantise(x_mx, x_raw, "x", 1, VECTOR_COLUMNS)
-        quantise(dy_mx, dy_raw, "dy", 0, VECTOR_COLUMNS)
-        quantise(dy_mx, dy_raw, "dy", 1, PART)
+        x_first = round_part(x_raw, "x", 0, PART)
+        nc.vector.transpose(out=ra_cols[:], in_=ra_rows[:])
+        nc.scalar.activation(out=rho[:], in_=ra_cols[:, 0:P:32], func=ACT.Abs_reciprocal_sqrt)
+        quantise(x_mx, x_first, 0)
+        quantise(x_mx, round_part(x_raw, "x", 1, VECTOR_COLUMNS), 1)
+        quantise(dy_mx, round_part(dy_raw, "dy", 0, VECTOR_COLUMNS), 0)
+        dy_second = round_part(dy_raw, "dy", 1, PART)
 
         def place(i):
-            return i % G, i // G
+            return i // HALVES, i % HALVES
 
         def product(bank, i, words, plane, moving):
             g, h = place(i)
@@ -153,39 +162,55 @@ def tile_rows_bsphere_kernel(tc, x, w1_words, w1_scales, w2_words, w2_scales, ra
                 out=dst[i][:], in0=bank[i][:], scalar=rho_of(i), in1=root[i][:], op0=ALU.mult, op1=ALU.mult
             )
 
-        def pieces(i):
-            return [slice(0, PART), slice(PART, N)] if i == TILES - 1 else [slice(0, N)]
+        def backward(i):
+            product(z2_bank[i], i, wo_sb, wo_plane, dy_mx)
 
-        def correction(i):
+        def unit_squared(i):
             nc.scalar.activation(out=unit2[i][:], in_=unit[i][:], func=ACT.Square)
-            for cols in pieces(i):
+
+        def finish(i, engine, pieces):
+            g, h = place(i)
+            for cols in pieces:
                 nc.vector.scalar_tensor_tensor(
                     out=minus[i][:, cols], in0=unit2[i][:, cols], scalar=1.0, in1=grad[i][:, cols],
                     op0=ALU.subtract, op1=ALU.mult,
                 )
-
-        def finish(i):
-            g, h = place(i)
-            for cols in pieces(i):
-                nc.vector.tensor_tensor(
-                    out=result[i][:, cols], in0=old_sb[:, HALVES * g + h, cols], in1=minus[i][:, cols], op=ALU.subtract
-                )
+            for cols in pieces:
+                engine.tensor_tensor(out=result[i][:, cols], in0=old_sb[g][:, h, cols], in1=minus[i][:, cols], op=ALU.subtract)
                 nc.sync.dma_start(out=out[g, P * h : P * (h + 1), cols], in_=result[i][:, cols])
 
+        whole = [slice(0, N)]
+        halves = [slice(0, PART), slice(PART, N)]
         forward(0)
         forward(1)
-        for step in range(TILES + 2):
-            if step < TILES:
-                squares(step)
-            if 1 <= step < TILES - 1:
-                forward(step + 1)
-            if step >= 2:
-                correction(step - 2)
-            if 1 <= step <= TILES:
-                product(z2_bank[step - 1], step - 1, wo_sb, wo_plane, dy_mx)
-                roots(step - 1)
-                times_root(unit, z1_bank, step - 1)
-            if step >= 2:
-                finish(step - 2)
-            if 1 <= step <= TILES:
-                times_root(grad, z2_bank, step - 1)
+        squares(0)
+        quantise(dy_mx, dy_second, 1)
+        squares(1)
+        forward(2)
+        backward(0)
+        roots(0)
+        times_root(unit, z1_bank, 0)
+        times_root(grad, z2_bank, 0)
+        squares(2)
+        forward(3)
+        unit_squared(0)
+        finish(0, nc.gpsimd, whole)
+        backward(1)
+        roots(1)
+        roots(2)
+        times_root(unit, z1_bank, 1)
+        times_root(grad, z2_bank, 1)
+        times_root(unit, z1_bank, 2)
+        squares(3)
+        unit_squared(1)
+        finish(1, nc.gpsimd, whole)
+        backward(2)
+        backward(3)
+        roots(3)
+        times_root(grad, z2_bank, 2)
+        times_root(unit, z1_bank, 3)
+        times_root(grad, z2_bank, 3)
+        unit_squared(2)
+        unit_squared(3)
+        finish(2, nc.vector, halves)
+        finish(3, nc.vector, halves)

@@ -111,7 +111,7 @@ def tile_rows_bsphere_kernel(tc, x, w1_words, w1_scales, w2_words, w2_scales, ra
         nc.scalar.activation(out=rho[:], in_=ra_cols[:, 0:P:32], func=ACT.Abs_reciprocal_sqrt)
         quantise(x_mx, x_first, 0)
         quantise(x_mx, round_part(x_raw, "x", 1, VECTOR_COLUMNS), 1)
-        quantise(dy_mx, round_part(dy_raw, "dy", 0, VECTOR_COLUMNS), 0)
+        quantise(dy_mx, round_part(dy_raw, "dy", 0, PART), 0)
         dy_second = round_part(dy_raw, "dy", 1, PART)
 
         def place(i):
@@ -145,6 +145,9 @@ def tile_rows_bsphere_kernel(tc, x, w1_words, w1_scales, w2_words, w2_scales, ra
             g, h = place(i)
             return rho[:, HALVES * g + h : HALVES * g + h + 1]
 
+        def ra_of(i):
+            return ra_cols[:, 32 * i : 32 * i + 1]
+
         def forward(i):
             product(z1_bank[i], i, w1_sb, w1_plane, x_mx)
             product(z2_bank[i], i, w2_sb, w2_plane, x_mx)
@@ -155,12 +158,10 @@ def tile_rows_bsphere_kernel(tc, x, w1_words, w1_scales, w2_words, w2_scales, ra
             nc.vector.tensor_tensor(out=radius2[i][:], in0=sq1[i][:], in1=sq2[i][:], op=ALU.add)
 
         def roots(i):
-            nc.scalar.activation(out=root[i][:], in_=radius2[i][:], func=ACT.Abs_reciprocal_sqrt, bias=1.0)
+            nc.scalar.activation(out=root[i][:], in_=radius2[i][:], func=ACT.Abs_reciprocal_sqrt, scale=ra_of(i), bias=ra_of(i))
 
         def times_root(dst, bank, i):
-            nc.vector.scalar_tensor_tensor(
-                out=dst[i][:], in0=bank[i][:], scalar=rho_of(i), in1=root[i][:], op0=ALU.mult, op1=ALU.mult
-            )
+            nc.vector.tensor_tensor(out=dst[i][:], in0=bank[i][:], in1=root[i][:], op=ALU.mult)
 
         def backward(i):
             product(z2_bank[i], i, wo_sb, wo_plane, dy_mx)

from contextlib import ExitStack

import concourse.mybir as mybir

G, D, M, N = 2, 256, 256, 512
FLOPS = 3 * 2 * G * D * M * N

F32 = mybir.dt.float32
BF16 = mybir.dt.bfloat16
I32 = mybir.dt.int32
U32 = mybir.dt.uint32
U8 = mybir.dt.uint8
FP8X4 = mybir.dt.float8_e4m3fn_x4
FP4X4 = mybir.dt.float4_e2m1fn_x4
ACT = mybir.ActivationFunctionType
ALU = mybir.AluOpType

P = 128
PACK = 4
ROWS = D // PACK
HALVES = M // P
TILES = G * HALVES
PART = N // 2
VECTOR_COLUMNS = 144


def tile_rows_bsphere_kernel(tc, x, w1_words, w1_scales, w2_words, w2_scales, ra, wo_words, wo_scales, dy, old, out):
    nc = tc.nc
    with ExitStack() as ctx:
        sb = ctx.enter_context(tc.tile_pool(name="sb", bufs=1))
        ps = ctx.enter_context(tc.psum_pool(name="ps", bufs=1))
        ctx.enter_context(tc.manual_schedule())

        x_raw = [sb.tile([P, PACK, PART], F32, name="x_raw%d" % k) for k in range(2)]
        dy_raw = [sb.tile([P, PACK, PART], F32, name="dy_raw%d" % k) for k in range(2)]
        old_sb = [sb.tile([P, HALVES, N], F32, name="old_sb%d" % g) for g in range(G)]
        ra_rows = sb.tile([P, P], F32, name="ra_rows", align_bytes=64)
        ra_cols = sb.tile([P, P], F32, name="ra_cols", align_bytes=64)
        rho = sb.tile([P, TILES], F32, name="rho")
        w_scales = sb.tile([P, 3 * M], U8, name="w_scales", align_bytes=64)
        w1_sb = sb.tile([P, 2 * M], U8, name="w1_sb", align_bytes=64)
        w2_sb = sb.tile([P, 2 * M], U8, name="w2_sb", align_bytes=64)
        wo_sb = sb.tile([P, 2 * M], U8, name="wo_sb", align_bytes=64)
        w1_plane, w2_plane, wo_plane = (w_scales[:, k * M : (k + 1) * M] for k in range(3))

        def load_rows(raw, src, part):
            rows = src.rearrange("g (p j) n -> (g p) j n", j=PACK)
            nc.sync.dma_start(out=raw[part][:], in_=rows[:, :, part * PART : (part + 1) * PART])

        def load_words(tile, words):
            nc.sync.dma_start(out=tile[:].bitcast(I32), in_=words.rearrange("g p b -> (g p) b").bitcast(I32))

        def load_plane(plane, scales, g):
            rows = scales.rearrange("g t m -> (g t) m").bitcast(I32)
            for q in (2 * g, 2 * g + 1):
                nc.sync.dma_start(out=plane[32 * q : 32 * q + 4, :].bitcast(I32), in_=rows[4 * q : 4 * q + 4, :])

        def load_old(g):
            nc.sync.dma_start(out=old_sb[g][:], in_=old[g].rearrange("(h p) n -> p h n", p=P))

        nc.vector.memset(ra_rows[:], 0.0)
        nc.vector.memset(w_scales[:].bitcast(I32), 0)
        load_rows(x_raw, x, 0)
        nc.sync.dma_start(
            out=ra_rows[0:P:32, :].rearrange("q (c i) -> q c i", i=32),
            in_=ra.rearrange("g (h q i) o -> q (g h) (i o)", q=4, i=32),
        )
        load_rows(x_raw, x, 1)
        load_words(w1_sb, w1_words)
        load_plane(w1_plane, w1_scales, 0)
        load_words(w2_sb, w2_words)
        load_plane(w2_plane, w2_scales, 0)
        load_rows(dy_raw, dy, 0)
        load_rows(dy_raw, dy, 1)
        load_words(wo_sb, wo_words)
        load_plane(wo_plane, wo_scales, 0)
        load_plane(w1_plane, w1_scales, 1)
        load_plane(w2_plane, w2_scales, 1)
        load_old(0)
        load_plane(wo_plane, wo_scales, 1)
        load_old(1)

        def interleave(copy, grouped, raw, c0, c1):
            copy(
                out=grouped[:, c0:c1, :].rearrange("p (c i) j -> p c j i", i=4),
                in_=raw[:, :, c0:c1].rearrange("p j (c i) -> p c j i", i=4),
            )

        def mx_operand(name):
            codes = sb.tile([P, N], U32, name=name + "_codes", align_bytes=64)
            scales = sb.tile([P, N], U8, name=name + "_scales", align_bytes=64)
            return codes, scales

        def round_part(raw, name, part, vector_columns):
            grouped = sb.tile([P, PART, PACK], BF16, name="%s_grouped%d" % (name, part), align_bytes=64)
            interleave(nc.vector.tensor_copy, grouped, raw[part], 0, vector_columns)
            if vector_columns < PART:
                interleave(nc.scalar.copy, grouped, raw[part], vector_columns, PART)
            return grouped

        def quantise(operand, grouped, part):
            codes, scales = operand
            cols = slice(part * PART, (part + 1) * PART)
            nc.vector.quantize_mx(
                out=codes[:, cols].bitcast(FP8X4), scales=scales[:, cols], in_=grouped[:].rearrange("p n j -> p (n j)")
            )

        x_mx, dy_mx = mx_operand("x"), mx_operand("dy")
        x_first = round_part(x_raw, "x", 0, PART)
        nc.vector.transpose(out=ra_cols[:], in_=ra_rows[:])
        nc.scalar.activation(out=rho[:], in_=ra_cols[:, 0:P:32], func=ACT.Abs_reciprocal_sqrt)
        quantise(x_mx, x_first, 0)
        quantise(x_mx, round_part(x_raw, "x", 1, VECTOR_COLUMNS), 1)
        quantise(dy_mx, round_part(dy_raw, "dy", 0, PART), 0)
        dy_second = round_part(dy_raw, "dy", 1, PART)

        def place(i):
            return i // HALVES, i % HALVES

        def product(bank, i, words, plane, moving):
            g, h = place(i)
            rows = slice(ROWS * g, ROWS * (g + 1))
            codes, scales = moving
            nc.tensor.matmul_mx(
                out=bank[:],
                lhsT=words[rows, 2 * P * h : 2 * P * (h + 1)].bitcast(FP4X4),
                lhsT_scale=plane[rows, P * h : P * (h + 1)],
                rhs=codes[rows, :].bitcast(FP8X4),
                rhs_scale=scales[rows, :],
                start=True,
                stop=True,
            )

        z1_bank = [ps.tile([P, N], F32, name="z1_bank%d" % i) for i in range(TILES)]
        z2_bank = [ps.tile([P, N], F32, name="z2_bank%d" % i) for i in range(TILES)]

        def work(name):
            return [sb.tile([P, N], F32, name="%s%d" % (name, i)) for i in range(TILES)]

        sq1, sq2, radius2, root, unit, grad, unit2, minus, result = (
            work(name) for name in ("sq1", "sq2", "radius2", "root", "unit", "grad", "unit2", "minus", "result")
        )

        def rho_of(i):
            g, h = place(i)
            return rho[:, HALVES * g + h : HALVES * g + h + 1]

        def ra_of(i):
            return ra_cols[:, 32 * i : 32 * i + 1]

        def forward(i):
            product(z1_bank[i], i, w1_sb, w1_plane, x_mx)
            product(z2_bank[i], i, w2_sb, w2_plane, x_mx)

        def squares(i):
            nc.scalar.activation(out=sq1[i][:], in_=z1_bank[i][:], func=ACT.Square, scale=rho_of(i))
            nc.scalar.activation(out=sq2[i][:], in_=z2_bank[i][:], func=ACT.Square, scale=rho_of(i))
            nc.vector.tensor_tensor(out=radius2[i][:], in0=sq1[i][:], in1=sq2[i][:], op=ALU.add)

        def roots(i):
            nc.scalar.activation(out=root[i][:], in_=radius2[i][:], func=ACT.Abs_reciprocal_sqrt, scale=ra_of(i), bias=ra_of(i))

        def times_root(dst, bank, i):
            nc.vector.tensor_tensor(out=dst[i][:], in0=bank[i][:], in1=root[i][:], op=ALU.mult)

        def backward(i):
            product(z2_bank[i], i, wo_sb, wo_plane, dy_mx)

        def unit_squared(i):
            nc.scalar.activation(out=unit2[i][:], in_=unit[i][:], func=ACT.Square)

        def finish(i, engine, pieces):
            g, h = place(i)
            for cols in pieces:
                nc.vector.scalar_tensor_tensor(
                    out=minus[i][:, cols], in0=unit2[i][:, cols], scalar=1.0, in1=grad[i][:, cols],
                    op0=ALU.subtract, op1=ALU.mult,
                )
            for cols in pieces:
                engine.tensor_tensor(out=result[i][:, cols], in0=old_sb[g][:, h, cols], in1=minus[i][:, cols], op=ALU.subtract)
                nc.sync.dma_start(out=out[g, P * h : P * (h + 1), cols], in_=result[i][:, cols])

        whole = [slice(0, N)]
        halves = [slice(0, PART), slice(PART, N)]
        forward(0)
        forward(1)
        squares(0)
        quantise(dy_mx, dy_second, 1)
        squares(1)
        forward(2)
        backward(0)
        roots(0)
        times_root(unit, z1_bank, 0)
        times_root(grad, z2_bank, 0)
        squares(2)
        forward(3)
        unit_squared(0)
        finish(0, nc.gpsimd, whole)
        backward(1)
        roots(1)
        roots(2)
        times_root(unit, z1_bank, 1)
        times_root(grad, z2_bank, 1)
        times_root(unit, z1_bank, 2)
        squares(3)
        unit_squared(1)
        finish(1, nc.gpsimd, whole)
        backward(2)
        backward(3)
        roots(3)
        times_root(grad, z2_bank, 2)
        times_root(unit, z1_bank, 3)
        times_root(grad, z2_bank, 3)
        unit_squared(2)
        unit_squared(3)
        finish(2, nc.vector, halves)
        finish(3, nc.vector, halves)
